import numpy as np
import ml_dtypes


def mxq(x, axis, fmt="e4m3"):
    dtype, down = {"e4m3": (ml_dtypes.float8_e4m3fn, 7), "e5m2": (ml_dtypes.float8_e5m2, 14)}[fmt]
    v = np.moveaxis(np.asarray(x, np.float32).astype(ml_dtypes.bfloat16).astype(np.float64), axis, -1)
    blocks = v.reshape(v.shape[:-1] + (-1, 32))
    amax = np.abs(blocks).max(-1, keepdims=True)
    byte = np.maximum(np.where(amax > 0, np.frexp(amax)[1] - 1 + 127, 0) - down, 1)
    scale = np.exp2(byte - 127.0)
    codes = (blocks / scale).astype(np.float32).astype(dtype).astype(np.float64)
    return np.moveaxis((codes * scale).reshape(v.shape), -1, axis)


WIDE = False


def mx_kscale(k):
    if not WIDE:
        return np.ones(k)
    levels = np.array([10, -10, 5, -5, 0])
    if k % 512:
        return np.exp2(np.random.permutation(np.resize(levels, k // 32))).repeat(32)
    a = np.empty((k // 512, 16))
    for p in range(k // 512):
        a[p, :8] = np.random.permutation(np.resize(levels, 8))
        for g in range(8):
            far = levels[np.abs(levels - a[p, g]) >= 10]
            a[p, g + 8] = far[np.random.randint(len(far))]
    return np.exp2(a.ravel()).repeat(32)


def f64(x):
    return np.asarray(x).astype(np.float64)


def striped(idx):
    return np.tile(idx.reshape(-1, 16).T, (8, 1)).astype(np.uint16)


def unstriped(offs):
    return offs[:16].T.reshape(-1).astype(np.int64)


def striped8(idx):
    return np.concatenate([x.reshape(-1, 16).T for x in idx]).astype(np.uint16)


def runs(offs, k):
    lists = np.stack([offs[16 * r : 16 * r + 16].T.reshape(-1) for r in range(8)]).astype(np.int64)
    return lists[np.arange(k) % 512 // 64]


def pack_weight(w):
    k, n = w.shape
    w = f64(np.asarray(w, np.float32).astype(ml_dtypes.bfloat16)).reshape(k // 32, 32, n)
    amax = np.abs(w).max(1)
    byte = np.clip(np.where(amax > 0, np.frexp(amax)[1] - 1 + 127 - 7, 1), 1, 254)
    scaled = (w * np.exp2(127.0 - byte)[:, None, :]).reshape(k, n).astype(np.float32)
    words = np.ascontiguousarray(scaled.reshape(k // 512, 128, 4, n).transpose(0, 1, 3, 2)).astype(ml_dtypes.float8_e4m3fn).view(np.uint8)
    return words, np.ascontiguousarray(byte.astype(np.uint8).reshape(k // 512, 16, n))


def unpack_weight(words, scales):
    g, p, n, _ = words.shape
    vals = np.ascontiguousarray(words).view(ml_dtypes.float8_e4m3fn).astype(np.float64) * np.repeat(np.exp2(scales.astype(np.float64) - 127.0), 8, axis=1)[..., None]
    return vals.transpose(0, 1, 3, 2).reshape(g * 512, n)


def relu(v):
    return np.maximum(v, 0.0)

def planes(y):
    n, m = y.shape
    v = y.astype(np.float32).astype(ml_dtypes.bfloat16).astype(np.float64).reshape(n // 32, 32, m)
    top = np.abs(v).max(1)
    byte = np.clip(np.where(top > 0, np.frexp(top)[1] - 1 + 127 - 7, 1), 1, 254)
    codes = (v * np.exp2(127.0 - byte)[:, None, :]).reshape(n, m).astype(np.float32).astype(ml_dtypes.float8_e4m3fn).view(np.uint8)
    words = codes.reshape(n // 512, 128, 4, m).transpose(0, 1, 3, 2)
    return np.ascontiguousarray(words), np.ascontiguousarray(byte.astype(np.uint8).reshape(n // 512, 16, m))


K, T, S, N, G, H = 512, 2048, 512, 512, 2048, 512


def setup_inputs():
    n = np.random.standard_normal
    s = mx_kscale(K)[:, None]
    u = mx_kscale(H)
    packed_xT = pack_weight(n((K, T)) * s)
    packed_dT = pack_weight(n((K, G)) / s)
    packed_w1 = pack_weight(n((H, N)) / np.sqrt(H) / u[:, None])
    return {
        "x_words": packed_xT[0],
        "x_scales": packed_xT[1],
        "d_words": packed_dT[0],
        "d_scales": packed_dT[1],
        "gn": (np.random.uniform(0.5, 1.5, (H, 1)) * u[:, None]).astype(np.float32),
        "w1_words": packed_w1[0],
        "w1_scales": packed_w1[1],
        "offs": striped(np.random.permutation(T)[:S]),
        "kidx": striped8(np.random.randint(0, G, (8, H))),
        "n1": striped8(np.stack([np.random.permutation(S) for _ in range(8)])),
    }


def reference(x_words, x_scales, d_words, d_scales, gn, w1_words, w1_scales, offs, kidx, n1):
    d_kidx = unpack_weight(d_words, d_scales)[np.arange(K)[:, None], runs(kidx, K)]
    xq = unpack_weight(x_words, x_scales)[:, unstriped(offs)]
    s = 0.0625 * (d_kidx.T @ xq)
    sq = (s) ** 2
    z = f64(gn) * ((s * relu(s)) / (sq + sq[np.arange(H)[:, None], runs(n1, H)] + 0.25))
    out_0 = unpack_weight(w1_words, w1_scales).T @ mxq(z, 0, "e4m3")
    return (out_0,) + planes(out_0)

@@ -1,0 +1,210 @@
+from contextlib import ExitStack
+
+import concourse.mybir as mybir
+
+K, T, S, N, G, H = 512, 2048, 512, 512, 2048, 512
+FLOPS = 2 * K * H * S + 2 * H * N * S
+
+F32 = mybir.dt.float32
+BF16 = mybir.dt.bfloat16
+I32 = mybir.dt.int32
+U32 = mybir.dt.uint32
+U16 = mybir.dt.uint16
+U8 = mybir.dt.uint8
+FP8X4 = mybir.dt.float8_e4m3fn_x4
+ACT = mybir.ActivationFunctionType
+ALU = mybir.AluOpType
+
+P = 128
+PACK = 4
+HALF = S // 2
+BLOCK = 128
+PIECES = ((0, 256), (256, 128), (384, 128))
+
+
+def tile_picked_scoreshare_none_po_kernel(
+    tc, x_words, x_scales, d_words, d_scales, gn, w1_words, w1_scales, offs, kidx, n1, out_0, out_1, out_2
+):
+    nc = tc.nc
+    with ExitStack() as ctx:
+        keep = ctx.enter_context(tc.tile_pool(name="keep", bufs=1))
+        reuse = ctx.enter_context(tc.tile_pool(name="reuse", bufs=1))
+        psum = ctx.enter_context(tc.psum_pool(name="psum", bufs=1))
+
+        def words_of(dram):
+            return dram[0].rearrange("p n t -> p (n t)").bitcast(I32)
+
+        kidx_sb = keep.tile([P, H // 16], U16, name="kidx_sb")
+        offs_sb = keep.tile([P, S // 16], U16, name="offs_sb")
+        n1_sb = keep.tile([P, S // 16], U16, name="n1_sb")
+        nc.sync.dma_start(kidx_sb[:], kidx)
+        nc.sync.dma_start(offs_sb[:], offs)
+        nc.sync.dma_start(n1_sb[:], n1)
+
+        d_table = keep.tile([P, G], U32, name="d_table", align_bytes=64)
+        x_table = keep.tile([P, T], U32, name="x_table", align_bytes=64)
+        nc.sync.dma_start(d_table[:].bitcast(I32), words_of(d_words))
+        nc.sync.dma_start(x_table[:].bitcast(I32), words_of(x_words))
+
+        ds_table = reuse.tile([P, G], U8, name="ds_table", align_bytes=64, offset=0)
+        nc.vector.memset(ds_table[:].bitcast(I32), 0)
+        for a in range(2):
+            nc.scalar.dma_start(ds_table[a:P:16, :].bitcast(I32), d_scales[0][a:16:2, :].bitcast(I32))
+        xs_table = keep.tile([P, T], U8, name="xs_table", align_bytes=64)
+        nc.vector.memset(xs_table[:].bitcast(I32), 0)
+        for a in range(4):
+            nc.scalar.dma_start(xs_table[a:P:32, :].bitcast(I32), x_scales[0][a:16:4, :].bitcast(I32))
+        w1s_raw = keep.tile([P, N], U8, name="w1s_raw", align_bytes=64)
+        nc.gpsimd.memset(w1s_raw[:].bitcast(I32), 0)
+        for a in range(4):
+            nc.gpsimd.dma_start(w1s_raw[a:P:32, :].bitcast(I32), w1_scales[0][a:16:4, :].bitcast(I32))
+
+        def deal(copy, dst, src):
+            copy(dst[:].rearrange("p (t m) -> p m t", t=PACK), src[:].rearrange("p (m t) -> p m t", t=PACK))
+
+        ds_picked = keep.tile([P, H], U8, name="ds_picked", align_bytes=64)
+        nc.vector.tensor_copy(ds_picked[:], ds_table[:].indirect(kidx_sb[:]))
+        w1_raw = reuse.tile([P, N], U32, name="w1_raw", align_bytes=64, offset=64)
+        nc.sync.dma_start(w1_raw[:].bitcast(I32), words_of(w1_words))
+        gn_sb = reuse.tile([P, PACK], F32, name="gn_sb", align_bytes=64, offset=0)
+        nc.sync.dma_start(gn_sb[:], gn.rearrange("(p t) o -> p (t o)", t=PACK))
+        ds_dealt = keep.tile([P, H], U8, name="ds_dealt", align_bytes=64)
+        deal(nc.vector.tensor_copy, ds_dealt, ds_picked)
+        for a in range(2):
+            nc.scalar.dma_start(ds_dealt[2 + a : P : 32, :].bitcast(I32), ds_dealt[16 + a : P : 32, :].bitcast(I32))
+
+        d_picked = keep.tile([P, H], U32, name="d_picked", align_bytes=64)
+        nc.vector.tensor_copy(d_picked[:], d_table[:].indirect(kidx_sb[:]))
+        d_dealt = keep.tile([P, H], U32, name="d_dealt", align_bytes=64)
+        deal(nc.vector.tensor_copy, d_dealt, d_picked)
+
+        w1_dealt = keep.tile([P, N], U32, name="w1_dealt", align_bytes=64)
+        deal(nc.scalar.copy, w1_dealt, w1_raw)
+
+        sq = [keep.tile([P, S], F32, name=f"sq{t}", align_bytes=64) for t in range(PACK)]
+        score = {}
+        for h in range(2):
+            entries = offs_sb[:, h * HALF // 16 : (h + 1) * HALF // 16]
+            xs_picked = keep.tile([P, HALF], U8, name=f"xs_picked{h}", align_bytes=64)
+            x_picked = keep.tile([P, HALF], U32, name=f"x_picked{h}", align_bytes=64)
+            nc.vector.tensor_copy(xs_picked[:], xs_table[:].indirect(entries))
+            nc.vector.tensor_copy(x_picked[:], x_table[:].indirect(entries))
+            for pair in range(2):
+                bank = psum.tile([P, 2, HALF], F32, name=f"score{h}{pair}")
+                score[h, pair] = bank
+                for e in range(2):
+                    cols = slice((2 * pair + e) * P, (2 * pair + e + 1) * P)
+                    nc.tensor.matmul_mx(
+                        out=bank[:, e, :],
+                        lhsT=d_dealt[:, cols].bitcast(FP8X4),
+                        lhsT_scale=ds_dealt[:, cols],
+                        rhs=x_picked[:].bitcast(FP8X4),
+                        rhs_scale=xs_picked[:],
+                        start=True,
+                        stop=True,
+                    )
+                for e in range(2):
+                    nc.scalar.activation(
+                        out=sq[2 * pair + e][:, h * HALF : (h + 1) * HALF], in_=bank[:, e, :], func=ACT.Square, scale=0.0625
+                    )
+
+        w1s_dealt = keep.tile([P, N], U8, name="w1s_dealt", align_bytes=64)
+        deal(nc.vector.tensor_copy, w1s_dealt, w1s_raw)
+
+        z = [keep.tile([P, PACK, HALF], BF16, name=f"z{h}", align_bytes=64) for h in range(2)]
+        den = {}
+
+        def denominators(h, pair):
+            entries = n1_sb[:, h * HALF // 16 : (h + 1) * HALF // 16]
+            other = keep.tile([P, 2, HALF], F32, name=f"other{h}{pair}", tag=f"stage{h}{pair}", align_bytes=64)
+            den[h, pair] = keep.tile([P, 2, HALF], F32, name=f"den{h}{pair}", tag=f"stage{h + 1}{pair}", align_bytes=64)
+            for e in range(2):
+                t = 2 * pair + e
+                if (h, pair) == (0, 0):
+                    nc.vector.tensor_copy(other[:, e, :], sq[t][:].indirect(entries))
+                else:
+                    nc.scalar.activation(out=other[:, e, :], in_=sq[t][:].indirect(entries), func=ACT.Copy)
+                nc.vector.scalar_tensor_tensor(
+                    out=den[h, pair][:, e, :], in0=other[:, e, :], scalar=0.25, in1=sq[t][:, h * HALF : (h + 1) * HALF], op0=ALU.add, op1=ALU.add
+                )
+
+        def shares(h, pair):
+            root = keep.tile([P, 2, HALF], F32, name=f"root{h}{pair}", align_bytes=64)
+            nc.scalar.activation(out=root[:], in_=den[h, pair][:], func=ACT.Abs_reciprocal_sqrt, scale=256.0)
+            u = keep.tile([P, 2, HALF], F32, name=f"u{h}{pair}", align_bytes=64)
+            nc.vector.scalar_tensor_tensor(out=u[:], in0=score[h, pair][:], scalar=0.0, in1=root[:], op0=ALU.max, op1=ALU.mult)
+            for e in range(2):
+                t = 2 * pair + e
+                nc.vector.scalar_tensor_tensor(
+                    out=z[h][:, t, :], in0=u[:, e, :], scalar=gn_sb[:, t : t + 1], in1=u[:, e, :], op0=ALU.mult, op1=ALU.mult
+                )
+
+        def weave(dst, src):
+            nc.vector.tensor_copy(dst[:].rearrange("p (c i) t -> p c t i", i=4), src.rearrange("p t (c i) -> p c t i", i=4))
+
+        out_scales = keep.tile([P, S], U8, name="out_scales", align_bytes=64)
+        out_rows = out_0.rearrange("(p t) j -> p t j", t=PACK)
+        result = {}
+        out_bank = {}
+
+        def second_product(j0, n):
+            h = j0 // HALF
+            woven = keep.tile([P, n, PACK], BF16, name=f"z_woven{j0}", align_bytes=64)
+            weave(woven, z[h][:, :, j0 - h * HALF : j0 - h * HALF + n])
+            codes = keep.tile([P, n], U32, name=f"z_codes{j0}", align_bytes=64)
+            scales = keep.tile([P, n], U8, name=f"z_scales{j0}", align_bytes=64)
+            nc.vector.quantize_mx(out=codes[:].bitcast(FP8X4), scales=scales[:], in_=woven[:].rearrange("p n t -> p (n t)"))
+            for b0 in range(0, n, BLOCK):
+                bank = psum.tile([P, PACK, BLOCK], F32, name=f"out{j0 + b0}")
+                out_bank[j0 + b0] = bank
+                for t in range(PACK):
+                    cols = slice(t * P, (t + 1) * P)
+                    nc.tensor.matmul_mx(
+                        out=bank[:, t, :],
+                        lhsT=w1_dealt[:, cols].bitcast(FP8X4),
+                        lhsT_scale=w1s_dealt[:, cols],
+                        rhs=codes[:, b0 : b0 + BLOCK].bitcast(FP8X4),
+                        rhs_scale=scales[:, b0 : b0 + BLOCK],
+                        start=True,
+                        stop=True,
+                    )
+
+        def store_result(j0, n):
+            result[j0] = keep.tile([P, PACK, n], F32, name=f"result{j0}", align_bytes=64)
+            for b0 in range(0, n, BLOCK):
+                nc.scalar.copy(result[j0][:, :, b0 : b0 + BLOCK], out_bank[j0 + b0][:])
+            nc.sync.dma_start(out_rows[:, :, j0 : j0 + n], result[j0][:])
+
+        def planes(j0, n):
+            woven = keep.tile([P, n, PACK], BF16, name=f"out_woven{j0}", align_bytes=64)
+            if j0 == 0:
+                for b0 in range(0, n, BLOCK):
+                    nc.scalar.copy(woven[:, b0 : b0 + BLOCK, :], out_bank[j0 + b0][:].rearrange("p t j -> p j t"))
+            else:
+                weave(woven, result[j0][:])
+            codes = keep.tile([P, n], U32, name=f"out_codes{j0}", align_bytes=64)
+            nc.vector.quantize_mx(
+                out=codes[:].bitcast(FP8X4), scales=out_scales[:, j0 : j0 + n], in_=woven[:].rearrange("p n t -> p (n t)")
+            )
+            nc.sync.dma_start(words_of(out_1)[:, j0 : j0 + n], codes[:].bitcast(I32))
+
+        denominators(0, 0)
+        denominators(0, 1)
+        shares(0, 0)
+        shares(0, 1)
+        denominators(1, 0)
+        second_product(*PIECES[0])
+        denominators(1, 1)
+        shares(1, 0)
+        shares(1, 1)
+        store_result(*PIECES[0])
+        second_product(*PIECES[1])
+        second_product(*PIECES[2])
+        planes(*PIECES[0])
+        store_result(*PIECES[1])
+        planes(*PIECES[1])
+        store_result(*PIECES[2])
+        planes(*PIECES[2])
+        for a in range(4):
+            queue = nc.sync if a % 2 else nc.scalar
+            queue.dma_start(out_2[0][a:16:4, :].bitcast(I32), out_scales[a:P:32, :].bitcast(I32))

@@ -38,78 +38,82 @@ def tile_picked_scoreshare_none_po_kernel(
         offs_sb = keep.tile([P, S // 16], U16, name="offs_sb")
         n1_sb = keep.tile([P, S // 16], U16, name="n1_sb")
         nc.sync.dma_start(kidx_sb[:], kidx)
-        nc.sync.dma_start(offs_sb[:], offs)
-        nc.sync.dma_start(n1_sb[:], n1)
 
-        d_table = keep.tile([P, G], U32, name="d_table", align_bytes=64)
-        x_table = keep.tile([P, T], U32, name="x_table", align_bytes=64)
-        nc.sync.dma_start(d_table[:].bitcast(I32), words_of(d_words))
-        nc.sync.dma_start(x_table[:].bitcast(I32), words_of(x_words))
-
-        ds_table = reuse.tile([P, G], U8, name="ds_table", align_bytes=64, offset=0)
-        nc.vector.memset(ds_table[:].bitcast(I32), 0)
-        for a in range(2):
-            nc.scalar.dma_start(ds_table[a:P:16, :].bitcast(I32), d_scales[0][a:16:2, :].bitcast(I32))
+        ds_table = keep.tile([P, G], U8, name="ds_table", align_bytes=64)
         xs_table = keep.tile([P, T], U8, name="xs_table", align_bytes=64)
+        d_table = keep.tile([P, G], U32, name="d_table", align_bytes=64)
+        x_table = reuse.tile([P, T], U32, name="x_table", align_bytes=64, offset=4096)
+        nc.vector.memset(ds_table[:].bitcast(I32), 0)
         nc.vector.memset(xs_table[:].bitcast(I32), 0)
+        nc.sync.dma_start(d_table[:, : G // 4].bitcast(I32), words_of(d_words)[:, : G // 4])
+        nc.sync.dma_start(ds_table[0:P:8, :].bitcast(I32), d_scales[0].bitcast(I32))
+        nc.sync.dma_start(d_table[:, G // 4 :].bitcast(I32), words_of(d_words)[:, G // 4 :])
+        nc.sync.dma_start(offs_sb[:], offs)
         for a in range(4):
             nc.scalar.dma_start(xs_table[a:P:32, :].bitcast(I32), x_scales[0][a:16:4, :].bitcast(I32))
-        w1s_raw = keep.tile([P, N], U8, name="w1s_raw", align_bytes=64)
-        nc.gpsimd.memset(w1s_raw[:].bitcast(I32), 0)
-        for a in range(4):
-            nc.gpsimd.dma_start(w1s_raw[a:P:32, :].bitcast(I32), w1_scales[0][a:16:4, :].bitcast(I32))
+        nc.sync.dma_start(x_table[:].bitcast(I32), words_of(x_words))
+        nc.sync.dma_start(n1_sb[:], n1)
 
-        def deal(copy, dst, src):
-            copy(dst[:].rearrange("p (t m) -> p m t", t=PACK), src[:].rearrange("p (m t) -> p m t", t=PACK))
+        def deal(dst, src, run, copy=nc.vector.tensor_copy):
+            copy(
+                dst[:].rearrange("p (t a b) -> p a t b", t=PACK, b=run), src[:].rearrange("p (a b t) -> p a t b", t=PACK, b=run)
+            )
 
-        ds_picked = keep.tile([P, H], U8, name="ds_picked", align_bytes=64)
+        ds_picked = reuse.tile([P, H], U8, name="ds_picked", align_bytes=64, offset=256)
         nc.vector.tensor_copy(ds_picked[:], ds_table[:].indirect(kidx_sb[:]))
-        w1_raw = reuse.tile([P, N], U32, name="w1_raw", align_bytes=64, offset=64)
-        nc.sync.dma_start(w1_raw[:].bitcast(I32), words_of(w1_words))
-        gn_sb = reuse.tile([P, PACK], F32, name="gn_sb", align_bytes=64, offset=0)
-        nc.sync.dma_start(gn_sb[:], gn.rearrange("(p t) o -> p (t o)", t=PACK))
         ds_dealt = keep.tile([P, H], U8, name="ds_dealt", align_bytes=64)
-        deal(nc.vector.tensor_copy, ds_dealt, ds_picked)
-        for a in range(2):
-            nc.scalar.dma_start(ds_dealt[2 + a : P : 32, :].bitcast(I32), ds_dealt[16 + a : P : 32, :].bitcast(I32))
+        deal(ds_dealt, ds_picked, 16)
+        for a in range(1, 4):
+            nc.scalar.dma_start(ds_dealt[a:P:32, :].bitcast(I32), ds_dealt[8 * a : P : 32, :].bitcast(I32))
+
+        w1s_raw = reuse.tile([P, N], U8, name="w1s_raw", align_bytes=64, offset=0)
+        gn_sb = reuse.tile([P, PACK], F32, name="gn_sb", align_bytes=64, offset=512)
+        w1_raw = reuse.tile([P, N], U32, name="w1_raw", align_bytes=64, offset=576)
+        nc.gpsimd.memset(w1s_raw[:].bitcast(I32), 0)
+        nc.sync.dma_start(gn_sb[:], gn.rearrange("(p t) o -> p (t o)", t=PACK))
+        nc.sync.dma_start(w1_raw[:].bitcast(I32), words_of(w1_words))
+        for a in range(4):
+            nc.sync.dma_start(w1s_raw[a:P:32, :].bitcast(I32), w1_scales[0][a:16:4, :].bitcast(I32))
 
         d_picked = keep.tile([P, H], U32, name="d_picked", align_bytes=64)
         nc.vector.tensor_copy(d_picked[:], d_table[:].indirect(kidx_sb[:]))
         d_dealt = keep.tile([P, H], U32, name="d_dealt", align_bytes=64)
-        deal(nc.vector.tensor_copy, d_dealt, d_picked)
+        deal(d_dealt, d_picked, 4)
 
         w1_dealt = keep.tile([P, N], U32, name="w1_dealt", align_bytes=64)
-        deal(nc.scalar.copy, w1_dealt, w1_raw)
+        deal(w1_dealt, w1_raw, 4, nc.scalar.copy)
 
         sq = [keep.tile([P, S], F32, name=f"sq{t}", align_bytes=64) for t in range(PACK)]
         score = {}
-        for h in range(2):
-            entries = offs_sb[:, h * HALF // 16 : (h + 1) * HALF // 16]
-            xs_picked = keep.tile([P, HALF], U8, name=f"xs_picked{h}", align_bytes=64)
-            x_picked = keep.tile([P, HALF], U32, name=f"x_picked{h}", align_bytes=64)
-            nc.vector.tensor_copy(xs_picked[:], xs_table[:].indirect(entries))
-            nc.vector.tensor_copy(x_picked[:], x_table[:].indirect(entries))
+        xs_picked = {}
+        for j0, n in ((0, HALF), (HALF, HALF)):
+            h, c0 = divmod(j0, HALF)
+            if c0 == 0:
+                xs_picked[h] = keep.tile([P, HALF], U8, name=f"xs_picked{h}", align_bytes=64)
+                nc.vector.tensor_copy(xs_picked[h][:], xs_table[:].indirect(offs_sb[:, j0 // 16 : (j0 + HALF) // 16]))
+                for pair in range(2):
+                    score[h, pair] = psum.tile([P, 2, HALF], F32, name=f"score{h}{pair}")
+            x_picked = keep.tile([P, n], U32, name=f"x_picked{j0}", align_bytes=64)
+            nc.vector.tensor_copy(x_picked[:], x_table[:].indirect(offs_sb[:, j0 // 16 : (j0 + n) // 16]))
             for pair in range(2):
-                bank = psum.tile([P, 2, HALF], F32, name=f"score{h}{pair}")
-                score[h, pair] = bank
                 for e in range(2):
                     cols = slice((2 * pair + e) * P, (2 * pair + e + 1) * P)
                     nc.tensor.matmul_mx(
-                        out=bank[:, e, :],
+                        out=score[h, pair][:, e, c0 : c0 + n],
                         lhsT=d_dealt[:, cols].bitcast(FP8X4),
                         lhsT_scale=ds_dealt[:, cols],
                         rhs=x_picked[:].bitcast(FP8X4),
-                        rhs_scale=xs_picked[:],
+                        rhs_scale=xs_picked[h][:, c0 : c0 + n],
                         start=True,
                         stop=True,
                     )
                 for e in range(2):
                     nc.scalar.activation(
-                        out=sq[2 * pair + e][:, h * HALF : (h + 1) * HALF], in_=bank[:, e, :], func=ACT.Square, scale=0.0625
+                        out=sq[2 * pair + e][:, j0 : j0 + n], in_=score[h, pair][:, e, c0 : c0 + n], func=ACT.Square, scale=0.0625
                     )
 
-        w1s_dealt = keep.tile([P, N], U8, name="w1s_dealt", align_bytes=64)
-        deal(nc.vector.tensor_copy, w1s_dealt, w1s_raw)
+        w1s_dealt = reuse.tile([P, N], U8, name="w1s_dealt", align_bytes=64, offset=4096)
+        deal(w1s_dealt, w1s_raw, 16)
 
         z = [keep.tile([P, PACK, HALF], BF16, name=f"z{h}", align_bytes=64) for h in range(2)]
         den = {}
@@ -140,7 +144,7 @@ def tile_picked_scoreshare_none_po_kernel(
                 )
 
         def weave(dst, src):
-            nc.vector.tensor_copy(dst[:].rearrange("p (c i) t -> p c t i", i=4), src.rearrange("p t (c i) -> p c t i", i=4))
+            nc.vector.tensor_copy(dst[:].rearrange("p (c i) t -> p c t i", i=2), src.rearrange("p t (c i) -> p c t i", i=2))
 
         out_scales = keep.tile([P, S], U8, name="out_scales", align_bytes=64)
         out_rows = out_0.rearrange("(p t) j -> p t j", t=PACK)

@@ -54,6 +54,11 @@ def tile_picked_scoreshare_none_po_kernel(
         nc.sync.dma_start(x_table[:].bitcast(I32), words_of(x_words))
         nc.sync.dma_start(n1_sb[:], n1)
 
+        warm_in = keep.tile([P, 1], F32, name="warm_in")
+        warm_out = keep.tile([P, 1], F32, name="warm_out")
+        nc.gpsimd.memset(warm_in[:], 1.0)
+        nc.scalar.activation(out=warm_out[:], in_=warm_in[:], func=ACT.Abs_reciprocal_sqrt)
+
         def deal(dst, src, run, copy=nc.vector.tensor_copy):
             copy(
                 dst[:].rearrange("p (t a b) -> p a t b", t=PACK, b=run), src[:].rearrange("p (a b t) -> p a t b", t=PACK, b=run)

@@ -19,6 +19,7 @@ P = 128
 PACK = 4
 HALF = S // 2
 BLOCK = 128
+BANK = 512
 PIECES = ((0, 256), (256, 128), (384, 128))
 
 
@@ -59,8 +60,8 @@ def tile_picked_scoreshare_none_po_kernel(
         nc.gpsimd.memset(warm_in[:], 1.0)
         nc.scalar.activation(out=warm_out[:], in_=warm_in[:], func=ACT.Abs_reciprocal_sqrt)
 
-        def deal(dst, src, run, copy=nc.vector.tensor_copy):
-            copy(
+        def deal(dst, src, run):
+            nc.vector.tensor_copy(
                 dst[:].rearrange("p (t a b) -> p a t b", t=PACK, b=run), src[:].rearrange("p (a b t) -> p a t b", t=PACK, b=run)
             )
 
@@ -85,51 +86,48 @@ def tile_picked_scoreshare_none_po_kernel(
         d_dealt = keep.tile([P, H], U32, name="d_dealt", align_bytes=64)
         deal(d_dealt, d_picked, 4)
 
-        w1_dealt = keep.tile([P, N], U32, name="w1_dealt", align_bytes=64)
-        deal(w1_dealt, w1_raw, 4, nc.scalar.copy)
-
         sq = [keep.tile([P, S], F32, name=f"sq{t}", align_bytes=64) for t in range(PACK)]
         score = {}
-        xs_picked = {}
-        for j0, n in ((0, HALF), (HALF, HALF)):
-            h, c0 = divmod(j0, HALF)
-            if c0 == 0:
-                xs_picked[h] = keep.tile([P, HALF], U8, name=f"xs_picked{h}", align_bytes=64)
-                nc.vector.tensor_copy(xs_picked[h][:], xs_table[:].indirect(offs_sb[:, j0 // 16 : (j0 + HALF) // 16]))
-                for pair in range(2):
-                    score[h, pair] = psum.tile([P, 2, HALF], F32, name=f"score{h}{pair}")
-            x_picked = keep.tile([P, n], U32, name=f"x_picked{j0}", align_bytes=64)
-            nc.vector.tensor_copy(x_picked[:], x_table[:].indirect(offs_sb[:, j0 // 16 : (j0 + n) // 16]))
+        xs_picked = keep.tile([P, S], U8, name="xs_picked", align_bytes=64)
+        nc.vector.tensor_copy(xs_picked[:], xs_table[:].indirect(offs_sb[:]))
+        for h in range(2):
             for pair in range(2):
-                for e in range(2):
-                    cols = slice((2 * pair + e) * P, (2 * pair + e + 1) * P)
+                score[h, pair] = psum.tile([P, 2, HALF], F32, name=f"score{h}{pair}")
+            for c0 in range(0, HALF, BLOCK):
+                j0 = h * HALF + c0
+                x_picked = keep.tile([P, BLOCK], U32, name=f"x_picked{j0}", align_bytes=64)
+                nc.vector.tensor_copy(x_picked[:], x_table[:].indirect(offs_sb[:, j0 // 16 : (j0 + BLOCK) // 16]))
+                for t in range(PACK):
+                    cols = slice(t * P, (t + 1) * P)
                     nc.tensor.matmul_mx(
-                        out=score[h, pair][:, e, c0 : c0 + n],
+                        out=score[h, t // 2][:, t % 2, c0 : c0 + BLOCK],
                         lhsT=d_dealt[:, cols].bitcast(FP8X4),
                         lhsT_scale=ds_dealt[:, cols],
                         rhs=x_picked[:].bitcast(FP8X4),
-                        rhs_scale=xs_picked[h][:, c0 : c0 + n],
+                        rhs_scale=xs_picked[:, j0 : j0 + BLOCK],
                         start=True,
                         stop=True,
                     )
-                for e in range(2):
-                    nc.scalar.activation(
-                        out=sq[2 * pair + e][:, j0 : j0 + n], in_=score[h, pair][:, e, c0 : c0 + n], func=ACT.Square, scale=0.0625
-                    )
+            for t in range(PACK):
+                nc.scalar.activation(
+                    out=sq[t][:, h * HALF : (h + 1) * HALF], in_=score[h, t // 2][:, t % 2, :], func=ACT.Square, scale=0.0625
+                )
 
         w1s_dealt = reuse.tile([P, N], U8, name="w1s_dealt", align_bytes=64, offset=4096)
         deal(w1s_dealt, w1s_raw, 16)
+        w1_dealt = reuse.tile([P, N], U32, name="w1_dealt", align_bytes=64, offset=4096 + N)
+        deal(w1_dealt, w1_raw, 4)
 
         z = [keep.tile([P, PACK, HALF], BF16, name=f"z{h}", align_bytes=64) for h in range(2)]
         den = {}
 
         def denominators(h, pair):
             entries = n1_sb[:, h * HALF // 16 : (h + 1) * HALF // 16]
-            other = keep.tile([P, 2, HALF], F32, name=f"other{h}{pair}", tag=f"stage{h}{pair}", align_bytes=64)
-            den[h, pair] = keep.tile([P, 2, HALF], F32, name=f"den{h}{pair}", tag=f"stage{h + 1}{pair}", align_bytes=64)
+            other = keep.tile([P, 2, HALF], F32, name=f"other{h}{pair}", align_bytes=64)
+            den[h, pair] = keep.tile([P, 2, HALF], F32, name=f"den{h}{pair}", align_bytes=64)
             for e in range(2):
                 t = 2 * pair + e
-                if (h, pair) == (0, 0):
+                if h == 0 and t < 3:
                     nc.vector.tensor_copy(other[:, e, :], sq[t][:].indirect(entries))
                 else:
                     nc.scalar.activation(out=other[:, e, :], in_=sq[t][:].indirect(entries), func=ACT.Copy)
@@ -148,8 +146,8 @@ def tile_picked_scoreshare_none_po_kernel(
                     out=z[h][:, t, :], in0=u[:, e, :], scalar=gn_sb[:, t : t + 1], in1=u[:, e, :], op0=ALU.mult, op1=ALU.mult
                 )
 
-        def weave(dst, src):
-            nc.vector.tensor_copy(dst[:].rearrange("p (c i) t -> p c t i", i=2), src.rearrange("p t (c i) -> p c t i", i=2))
+        def weave(dst, src, copy=nc.vector.tensor_copy):
+            copy(dst[:].rearrange("p (c i) t -> p c t i", i=2), src.rearrange("p t (c i) -> p c t i", i=2))
 
         out_scales = keep.tile([P, S], U8, name="out_scales", align_bytes=64)
         out_rows = out_0.rearrange("(p t) j -> p t j", t=PACK)
@@ -159,38 +157,35 @@ def tile_picked_scoreshare_none_po_kernel(
         def second_product(j0, n):
             h = j0 // HALF
             woven = keep.tile([P, n, PACK], BF16, name=f"z_woven{j0}", align_bytes=64)
-            weave(woven, z[h][:, :, j0 - h * HALF : j0 - h * HALF + n])
+            weave(woven, z[h][:, :, j0 - h * HALF : j0 - h * HALF + n], nc.scalar.copy if j0 == 0 else nc.vector.tensor_copy)
             codes = keep.tile([P, n], U32, name=f"z_codes{j0}", align_bytes=64)
             scales = keep.tile([P, n], U8, name=f"z_scales{j0}", align_bytes=64)
             nc.vector.quantize_mx(out=codes[:].bitcast(FP8X4), scales=scales[:], in_=woven[:].rearrange("p n t -> p (n t)"))
-            for b0 in range(0, n, BLOCK):
-                bank = psum.tile([P, PACK, BLOCK], F32, name=f"out{j0 + b0}")
-                out_bank[j0 + b0] = bank
-                for t in range(PACK):
-                    cols = slice(t * P, (t + 1) * P)
-                    nc.tensor.matmul_mx(
-                        out=bank[:, t, :],
-                        lhsT=w1_dealt[:, cols].bitcast(FP8X4),
-                        lhsT_scale=w1s_dealt[:, cols],
-                        rhs=codes[:, b0 : b0 + BLOCK].bitcast(FP8X4),
-                        rhs_scale=scales[:, b0 : b0 + BLOCK],
-                        start=True,
-                        stop=True,
-                    )
+            per_bank = BANK // n
+            for t in range(PACK):
+                if t % per_bank == 0:
+                    out_bank[j0, t] = psum.tile([P, per_bank, n], F32, name=f"out{j0}_{t}")
+                cols = slice(t * P, (t + 1) * P)
+                nc.tensor.matmul_mx(
+                    out=out_bank[j0, t - t % per_bank][:, t % per_bank, :],
+                    lhsT=w1_dealt[:, cols].bitcast(FP8X4),
+                    lhsT_scale=w1s_dealt[:, cols],
+                    rhs=codes[:].bitcast(FP8X4),
+                    rhs_scale=scales[:],
+                    start=True,
+                    stop=True,
+                )
 
         def store_result(j0, n):
             result[j0] = keep.tile([P, PACK, n], F32, name=f"result{j0}", align_bytes=64)
-            for b0 in range(0, n, BLOCK):
-                nc.scalar.copy(result[j0][:, :, b0 : b0 + BLOCK], out_bank[j0 + b0][:])
-            nc.sync.dma_start(out_rows[:, :, j0 : j0 + n], result[j0][:])
+            per_bank = BANK // n
+            for t0 in range(0, PACK, per_bank):
+                nc.scalar.copy(result[j0][:, t0 : t0 + per_bank, :], out_bank[j0, t0][:])
+                nc.sync.dma_start(out_rows[:, t0 : t0 + per_bank, j0 : j0 + n], result[j0][:, t0 : t0 + per_bank, :])
 
         def planes(j0, n):
             woven = keep.tile([P, n, PACK], BF16, name=f"out_woven{j0}", align_bytes=64)
-            if j0 == 0:
-                for b0 in range(0, n, BLOCK):
-                    nc.scalar.copy(woven[:, b0 : b0 + BLOCK, :], out_bank[j0 + b0][:].rearrange("p t j -> p j t"))
-            else:
-                weave(woven, result[j0][:])
+            weave(woven, result[j0][:])
             codes = keep.tile([P, n], U32, name=f"out_codes{j0}", align_bytes=64)
             nc.vector.quantize_mx(
                 out=codes[:].bitcast(FP8X4), scales=out_scales[:, j0 : j0 + n], in_=woven[:].rearrange("p n t -> p (n t)")

from contextlib import ExitStack

import concourse.mybir as mybir

K, T, S, N, G, H = 512, 2048, 512, 512, 2048, 512
FLOPS = 2 * K * H * S + 2 * H * N * S

F32 = mybir.dt.float32
BF16 = mybir.dt.bfloat16
I32 = mybir.dt.int32
U32 = mybir.dt.uint32
U16 = mybir.dt.uint16
U8 = mybir.dt.uint8
FP8X4 = mybir.dt.float8_e4m3fn_x4
ACT = mybir.ActivationFunctionType
ALU = mybir.AluOpType

P = 128
PACK = 4
HALF = S // 2
BLOCK = 128
BANK = 512
PIECES = ((0, 256), (256, 128), (384, 128))


def tile_picked_scoreshare_none_po_kernel(
    tc, x_words, x_scales, d_words, d_scales, gn, w1_words, w1_scales, offs, kidx, n1, out_0, out_1, out_2
):
    nc = tc.nc
    with ExitStack() as ctx:
        keep = ctx.enter_context(tc.tile_pool(name="keep", bufs=1))
        reuse = ctx.enter_context(tc.tile_pool(name="reuse", bufs=1))
        psum = ctx.enter_context(tc.psum_pool(name="psum", bufs=1))

        def words_of(dram):
            return dram[0].rearrange("p n t -> p (n t)").bitcast(I32)

        kidx_sb = keep.tile([P, H // 16], U16, name="kidx_sb")
        offs_sb = keep.tile([P, S // 16], U16, name="offs_sb")
        n1_sb = keep.tile([P, S // 16], U16, name="n1_sb")
        nc.sync.dma_start(kidx_sb[:], kidx)

        ds_table = keep.tile([P, G], U8, name="ds_table", align_bytes=64)
        xs_table = keep.tile([P, T], U8, name="xs_table", align_bytes=64)
        d_table = keep.tile([P, G], U32, name="d_table", align_bytes=64)
        x_table = reuse.tile([P, T], U32, name="x_table", align_bytes=64, offset=4096)
        nc.vector.memset(ds_table[:].bitcast(I32), 0)
        nc.vector.memset(xs_table[:].bitcast(I32), 0)
        nc.sync.dma_start(d_table[:, : G // 4].bitcast(I32), words_of(d_words)[:, : G // 4])
        nc.sync.dma_start(ds_table[0:P:8, :].bitcast(I32), d_scales[0].bitcast(I32))
        nc.sync.dma_start(d_table[:, G // 4 :].bitcast(I32), words_of(d_words)[:, G // 4 :])
        nc.sync.dma_start(offs_sb[:], offs)
        for a in range(4):
            nc.scalar.dma_start(xs_table[a:P:32, :].bitcast(I32), x_scales[0][a:16:4, :].bitcast(I32))
        nc.sync.dma_start(x_table[:].bitcast(I32), words_of(x_words))
        nc.sync.dma_start(n1_sb[:], n1)

        warm_in = keep.tile([P, 1], F32, name="warm_in")
        warm_out = keep.tile([P, 1], F32, name="warm_out")
        nc.gpsimd.memset(warm_in[:], 1.0)
        nc.scalar.activation(out=warm_out[:], in_=warm_in[:], func=ACT.Abs_reciprocal_sqrt)

        def deal(dst, src, run):
            nc.vector.tensor_copy(
                dst[:].rearrange("p (t a b) -> p a t b", t=PACK, b=run), src[:].rearrange("p (a b t) -> p a t b", t=PACK, b=run)
            )

        ds_picked = reuse.tile([P, H], U8, name="ds_picked", align_bytes=64, offset=256)
        nc.vector.tensor_copy(ds_picked[:], ds_table[:].indirect(kidx_sb[:]))
        ds_dealt = keep.tile([P, H], U8, name="ds_dealt", align_bytes=64)
        deal(ds_dealt, ds_picked, 16)
        for a in range(1, 4):
            nc.scalar.dma_start(ds_dealt[a:P:32, :].bitcast(I32), ds_dealt[8 * a : P : 32, :].bitcast(I32))

        w1s_raw = reuse.tile([P, N], U8, name="w1s_raw", align_bytes=64, offset=0)
        gn_sb = reuse.tile([P, PACK], F32, name="gn_sb", align_bytes=64, offset=512)
        w1_raw = reuse.tile([P, N], U32, name="w1_raw", align_bytes=64, offset=576)
        nc.gpsimd.memset(w1s_raw[:].bitcast(I32), 0)
        nc.sync.dma_start(gn_sb[:], gn.rearrange("(p t) o -> p (t o)", t=PACK))
        nc.sync.dma_start(w1_raw[:].bitcast(I32), words_of(w1_words))
        for a in range(4):
            nc.sync.dma_start(w1s_raw[a:P:32, :].bitcast(I32), w1_scales[0][a:16:4, :].bitcast(I32))

        d_picked = keep.tile([P, H], U32, name="d_picked", align_bytes=64)
        nc.vector.tensor_copy(d_picked[:], d_table[:].indirect(kidx_sb[:]))
        d_dealt = keep.tile([P, H], U32, name="d_dealt", align_bytes=64)
        deal(d_dealt, d_picked, 4)

        sq = [keep.tile([P, S], F32, name=f"sq{t}", align_bytes=64) for t in range(PACK)]
        score = {}
        xs_picked = keep.tile([P, S], U8, name="xs_picked", align_bytes=64)
        nc.vector.tensor_copy(xs_picked[:], xs_table[:].indirect(offs_sb[:]))
        for h in range(2):
            for pair in range(2):
                score[h, pair] = psum.tile([P, 2, HALF], F32, name=f"score{h}{pair}")
            for c0 in range(0, HALF, BLOCK):
                j0 = h * HALF + c0
                x_picked = keep.tile([P, BLOCK], U32, name=f"x_picked{j0}", align_bytes=64)
                nc.vector.tensor_copy(x_picked[:], x_table[:].indirect(offs_sb[:, j0 // 16 : (j0 + BLOCK) // 16]))
                for t in range(PACK):
                    cols = slice(t * P, (t + 1) * P)
                    nc.tensor.matmul_mx(
                        out=score[h, t // 2][:, t % 2, c0 : c0 + BLOCK],
                        lhsT=d_dealt[:, cols].bitcast(FP8X4),
                        lhsT_scale=ds_dealt[:, cols],
                        rhs=x_picked[:].bitcast(FP8X4),
                        rhs_scale=xs_picked[:, j0 : j0 + BLOCK],
                        start=True,
                        stop=True,
                    )
            for t in range(PACK):
                nc.scalar.activation(
                    out=sq[t][:, h * HALF : (h + 1) * HALF], in_=score[h, t // 2][:, t % 2, :], func=ACT.Square, scale=0.0625
                )

        w1s_dealt = reuse.tile([P, N], U8, name="w1s_dealt", align_bytes=64, offset=4096)
        deal(w1s_dealt, w1s_raw, 16)
        w1_dealt = reuse.tile([P, N], U32, name="w1_dealt", align_bytes=64, offset=4096 + N)
        deal(w1_dealt, w1_raw, 4)

        z = [keep.tile([P, PACK, HALF], BF16, name=f"z{h}", align_bytes=64) for h in range(2)]
        den = {}

        def denominators(h, pair):
            entries = n1_sb[:, h * HALF // 16 : (h + 1) * HALF // 16]
            other = keep.tile([P, 2, HALF], F32, name=f"other{h}{pair}", align_bytes=64)
            den[h, pair] = keep.tile([P, 2, HALF], F32, name=f"den{h}{pair}", align_bytes=64)
            for e in range(2):
                t = 2 * pair + e
                if h == 0 and t < 3:
                    nc.vector.tensor_copy(other[:, e, :], sq[t][:].indirect(entries))
                else:
                    nc.scalar.activation(out=other[:, e, :], in_=sq[t][:].indirect(entries), func=ACT.Copy)
                nc.vector.scalar_tensor_tensor(
                    out=den[h, pair][:, e, :], in0=other[:, e, :], scalar=0.25, in1=sq[t][:, h * HALF : (h + 1) * HALF], op0=ALU.add, op1=ALU.add
                )

        def shares(h, pair):
            root = keep.tile([P, 2, HALF], F32, name=f"root{h}{pair}", align_bytes=64)
            nc.scalar.activation(out=root[:], in_=den[h, pair][:], func=ACT.Abs_reciprocal_sqrt, scale=256.0)
            u = keep.tile([P, 2, HALF], F32, name=f"u{h}{pair}", align_bytes=64)
            nc.vector.scalar_tensor_tensor(out=u[:], in0=score[h, pair][:], scalar=0.0, in1=root[:], op0=ALU.max, op1=ALU.mult)
            for e in range(2):
                t = 2 * pair + e
                nc.vector.scalar_tensor_tensor(
                    out=z[h][:, t, :], in0=u[:, e, :], scalar=gn_sb[:, t : t + 1], in1=u[:, e, :], op0=ALU.mult, op1=ALU.mult
                )

        def weave(dst, src, copy=nc.vector.tensor_copy):
            copy(dst[:].rearrange("p (c i) t -> p c t i", i=2), src.rearrange("p t (c i) -> p c t i", i=2))

        out_scales = keep.tile([P, S], U8, name="out_scales", align_bytes=64)
        out_rows = out_0.rearrange("(p t) j -> p t j", t=PACK)
        result = {}
        out_bank = {}

        def second_product(j0, n):
            h = j0 // HALF
            woven = keep.tile([P, n, PACK], BF16, name=f"z_woven{j0}", align_bytes=64)
            weave(woven, z[h][:, :, j0 - h * HALF : j0 - h * HALF + n], nc.scalar.copy if j0 == 0 else nc.vector.tensor_copy)
            codes = keep.tile([P, n], U32, name=f"z_codes{j0}", align_bytes=64)
            scales = keep.tile([P, n], U8, name=f"z_scales{j0}", align_bytes=64)
            nc.vector.quantize_mx(out=codes[:].bitcast(FP8X4), scales=scales[:], in_=woven[:].rearrange("p n t -> p (n t)"))
            per_bank = BANK // n
            for t in range(PACK):
                if t % per_bank == 0:
                    out_bank[j0, t] = psum.tile([P, per_bank, n], F32, name=f"out{j0}_{t}")
                cols = slice(t * P, (t + 1) * P)
                nc.tensor.matmul_mx(
                    out=out_bank[j0, t - t % per_bank][:, t % per_bank, :],
                    lhsT=w1_dealt[:, cols].bitcast(FP8X4),
                    lhsT_scale=w1s_dealt[:, cols],
                    rhs=codes[:].bitcast(FP8X4),
                    rhs_scale=scales[:],
                    start=True,
                    stop=True,
                )

        def store_result(j0, n):
            result[j0] = keep.tile([P, PACK, n], F32, name=f"result{j0}", align_bytes=64)
            per_bank = BANK // n
            for t0 in range(0, PACK, per_bank):
                nc.scalar.copy(result[j0][:, t0 : t0 + per_bank, :], out_bank[j0, t0][:])
                nc.sync.dma_start(out_rows[:, t0 : t0 + per_bank, j0 : j0 + n], result[j0][:, t0 : t0 + per_bank, :])

        def planes(j0, n):
            woven = keep.tile([P, n, PACK], BF16, name=f"out_woven{j0}", align_bytes=64)
            weave(woven, result[j0][:])
            codes = keep.tile([P, n], U32, name=f"out_codes{j0}", align_bytes=64)
            nc.vector.quantize_mx(
                out=codes[:].bitcast(FP8X4), scales=out_scales[:, j0 : j0 + n], in_=woven[:].rearrange("p n t -> p (n t)")
            )
            nc.sync.dma_start(words_of(out_1)[:, j0 : j0 + n], codes[:].bitcast(I32))

        denominators(0, 0)
        denominators(0, 1)
        shares(0, 0)
        shares(0, 1)
        denominators(1, 0)
        second_product(*PIECES[0])
        denominators(1, 1)
        shares(1, 0)
        shares(1, 1)
        store_result(*PIECES[0])
        second_product(*PIECES[1])
        second_product(*PIECES[2])
        planes(*PIECES[0])
        store_result(*PIECES[1])
        planes(*PIECES[1])
        store_result(*PIECES[2])
        planes(*PIECES[2])
        for a in range(4):
            queue = nc.sync if a % 2 else nc.scalar
            queue.dma_start(out_2[0][a:16:4, :].bitcast(I32), out_scales[a:P:32, :].bitcast(I32))
